import numpy as np
import ml_dtypes


def mxq(x, axis, fmt="e4m3"):
    dtype, down = {"e4m3": (ml_dtypes.float8_e4m3fn, 7), "e5m2": (ml_dtypes.float8_e5m2, 14)}[fmt]
    v = np.moveaxis(np.asarray(x, np.float32).astype(ml_dtypes.bfloat16).astype(np.float64), axis, -1)
    blocks = v.reshape(v.shape[:-1] + (-1, 32))
    amax = np.abs(blocks).max(-1, keepdims=True)
    byte = np.maximum(np.where(amax > 0, np.frexp(amax)[1] - 1 + 127, 0) - down, 1)
    scale = np.exp2(byte - 127.0)
    codes = (blocks / scale).astype(np.float32).astype(dtype).astype(np.float64)
    return np.moveaxis((codes * scale).reshape(v.shape), -1, axis)


WIDE = False


def mx_kscale(k):
    if not WIDE:
        return np.ones(k)
    levels = np.array([10, -10, 5, -5, 0])
    if k % 512:
        return np.exp2(np.random.permutation(np.resize(levels, k // 32))).repeat(32)
    a = np.empty((k // 512, 16))
    for p in range(k // 512):
        a[p, :8] = np.random.permutation(np.resize(levels, 8))
        for g in range(8):
            far = levels[np.abs(levels - a[p, g]) >= 10]
            a[p, g + 8] = far[np.random.randint(len(far))]
    return np.exp2(a.ravel()).repeat(32)


def f64(x):
    return np.asarray(x).astype(np.float64)


def striped(idx):
    return np.tile(idx.reshape(-1, 16).T, (8, 1)).astype(np.uint16)


def unstriped(offs):
    return offs[:16].T.reshape(-1).astype(np.int64)


def pack_weight(w):
    k, n = w.shape
    w = f64(np.asarray(w, np.float32).astype(ml_dtypes.bfloat16)).reshape(k // 32, 32, n)
    amax = np.abs(w).max(1)
    byte = np.clip(np.where(amax > 0, np.frexp(amax)[1] - 1 + 127 - 7, 1), 1, 254)
    scaled = (w * np.exp2(127.0 - byte)[:, None, :]).reshape(k, n).astype(np.float32)
    words = np.ascontiguousarray(scaled.reshape(k // 512, 128, 4, n).transpose(0, 1, 3, 2)).astype(ml_dtypes.float8_e4m3fn).view(np.uint8)
    return words, np.ascontiguousarray(byte.astype(np.uint8).reshape(k // 512, 16, n))


def unpack_weight(words, scales):
    g, p, n, _ = words.shape
    vals = np.ascontiguousarray(words).view(ml_dtypes.float8_e4m3fn).astype(np.float64) * np.repeat(np.exp2(scales.astype(np.float64) - 127.0), 8, axis=1)[..., None]
    return vals.transpose(0, 1, 3, 2).reshape(g * 512, n)


E2M1 = np.array([0.0, 0.5, 1.0, 1.5, 2.0, 3.0, 4.0, 6.0, -0.0, -0.5, -1.0, -1.5, -2.0, -3.0, -4.0, -6.0])


def pack_fp4(w):
    k, n = w.shape
    w = f64(np.asarray(w, np.float32).astype(ml_dtypes.bfloat16)).reshape(k // 32, 32, n)
    amax = np.abs(w).max(1)
    mant, ex = np.frexp(amax / 6.0)
    byte = np.clip(np.where(amax > 0, np.where(mant > 0.5, ex, ex - 1) + 127, 1), 1, 254)
    scaled = (w * np.exp2(127.0 - byte)[:, None, :]).reshape(k, n).astype(np.float32)
    c = np.ascontiguousarray(scaled.reshape(k // 512, 128, 4, n).transpose(0, 1, 3, 2)).astype(ml_dtypes.float4_e2m1fn).view(np.uint8) & 0xF
    words = (c[..., 0::2] | (c[..., 1::2] << 4)).reshape(k // 512, 128, 2 * n)
    return np.ascontiguousarray(words), np.ascontiguousarray(byte.astype(np.uint8).reshape(k // 512, 16, n))


def unpack_fp4(words, scales):
    g, _, n = scales.shape
    words = np.ascontiguousarray(words).reshape(g, 128, n, 2)
    nib = np.empty((g, 128, n, 4), np.uint8)
    nib[..., 0::2] = words & 0xF
    nib[..., 1::2] = words >> 4
    vals = E2M1[nib] * np.repeat(np.exp2(scales.astype(np.float64) - 127.0), 8, axis=1)[..., None]
    return vals.transpose(0, 1, 3, 2).reshape(g * 512, n)


def planes(y):
    n, m = y.shape
    v = y.astype(np.float32).astype(ml_dtypes.bfloat16).astype(np.float64).reshape(n // 32, 32, m)
    top = np.abs(v).max(1)
    byte = np.clip(np.where(top > 0, np.frexp(top)[1] - 1 + 127 - 7, 1), 1, 254)
    codes = (v * np.exp2(127.0 - byte)[:, None, :]).reshape(n, m).astype(np.float32).astype(ml_dtypes.float8_e4m3fn).view(np.uint8)
    words = codes.reshape(n // 512, 128, 4, m).transpose(0, 1, 3, 2)
    return np.ascontiguousarray(words), np.ascontiguousarray(byte.astype(np.uint8).reshape(n // 512, 16, m))


K, T, S, N, H, U = 512, 1024, 512, 512, 512, 1024


def setup_inputs():
    n = np.random.standard_normal
    s = mx_kscale(K)[:, None]
    u = mx_kscale(H)
    packed_xT = pack_weight(n((K, T)) * s)
    packed_w1 = pack_fp4(n((K, N)) / np.sqrt(K) / s)
    packed_w2 = pack_fp4(n((K, N)) / np.sqrt(K) / s)
    packed_w3 = pack_fp4(n((H, N)) / np.sqrt(H) / u[:, None])
    return {
        "x_words": packed_xT[0],
        "x_scales": packed_xT[1],
        "w1_words": packed_w1[0],
        "w1_scales": packed_w1[1],
        "w2_words": packed_w2[0],
        "w2_scales": packed_w2[1],
        "unit": (np.random.uniform(0.6, 1.4, (H, 1)) * u[:, None]).astype(np.float32),
        "w3_words": packed_w3[0],
        "w3_scales": packed_w3[1],
        "offs": striped(np.random.permutation(T)[:S]),
        "ask1": striped(np.random.permutation(np.concatenate([np.arange(S), np.random.randint(0, S, U - S)]))),
        "ask2": striped(np.random.permutation(np.concatenate([np.arange(S), np.random.randint(0, S, U - S)]))),
    }


def reference(x_words, x_scales, w1_words, w1_scales, w2_words, w2_scales, unit, w3_words, w3_scales, offs, ask1, ask2):
    xq = unpack_weight(x_words, x_scales)[:, unstriped(offs)]
    y = unpack_fp4(w1_words, w1_scales).T @ xq
    ya = y[:, unstriped(ask1)]
    z1 = unpack_fp4(w2_words, w2_scales).T @ xq
    zb_ = z1[:, unstriped(ask2)]
    yb_ = y[:, unstriped(ask2)]
    za = z1[:, unstriped(ask1)]
    hid = f64(unit) * np.minimum(ya + zb_, yb_ + za)
    out_0 = unpack_fp4(w3_words, w3_scales).T @ mxq(hid, 0, "e4m3")
    return (out_0,) + planes(out_0)

@@ -1,0 +1,193 @@
+from contextlib import ExitStack
+
+import concourse.mybir as mybir
+
+K, T, S, N, H, U = 512, 1024, 512, 512, 512, 1024
+FLOPS = 2 * K * N * S * 2 + 2 * H * N * U
+
+F32 = mybir.dt.float32
+BF16 = mybir.dt.bfloat16
+I32 = mybir.dt.int32
+U32 = mybir.dt.uint32
+U16 = mybir.dt.uint16
+U8 = mybir.dt.uint8
+FP8X4 = mybir.dt.float8_e4m3fn_x4
+FP4X4 = mybir.dt.float4_e2m1fn_x4
+ALU = mybir.AluOpType
+ACT = mybir.ActivationFunctionType
+
+P = 128
+PACK = 4
+LANES = 16
+UNIT = 128
+CHUNKS = (256, 256, 256, 128, 128)
+RUN = 2
+
+
+def tile_picked_ypeerlo_cmb_po_kernel(
+    tc, x_words, x_scales, w1_words, w1_scales, w2_words, w2_scales, unit, w3_words, w3_scales,
+    offs, ask1, ask2, out_0, out_1, out_2,
+):
+    nc = tc.nc
+    with ExitStack() as ctx:
+        lists = ctx.enter_context(tc.tile_pool(name="lists", bufs=1))
+        keep = ctx.enter_context(tc.tile_pool(name="keep", bufs=1))
+        ring = ctx.enter_context(tc.tile_pool(name="ring", bufs=2))
+        psum = ctx.enter_context(tc.psum_pool(name="psum", bufs=1))
+
+        def load_scale_rows(queue, plane, rows):
+            for q in range(4):
+                queue.dma_start(
+                    out=plane[32 * q : 32 * q + 4, :].bitcast(I32),
+                    in_=rows[0, 4 * q : 4 * q + 4, :].bitcast(I32),
+                )
+
+        offs_t = lists.tile([P, S // LANES], U16, name="offs_t")
+        ask1_t = lists.tile([P, U // LANES], U16, name="ask1_t")
+        ask2_t = lists.tile([P, U // LANES], U16, name="ask2_t")
+
+        xw = keep.tile([P, T], U32, name="xw", align_bytes=64)
+        xs = keep.tile([P, T], U8, name="xs", align_bytes=64)
+        raw_w = [keep.tile([P, 2 * N], U8, name="raw_w%d" % i, align_bytes=64) for i in range(3)]
+        raw_s = [keep.tile([P, N], U8, name="raw_s%d" % i, align_bytes=64) for i in range(3)]
+        w_words = (w1_words, w2_words, w3_words)
+        w_scales = (w1_scales, w2_scales, w3_scales)
+        unit_t = keep.tile([P, PACK], F32, name="unit_t")
+
+        nc.vector.memset(xs[:].bitcast(I32), 0)
+        for i in range(3):
+            nc.vector.memset(raw_s[i][:].bitcast(I32), 0)
+
+        nc.sync.dma_start(out=offs_t[:], in_=offs)
+        load_scale_rows(nc.sync, xs, x_scales)
+        nc.sync.dma_start(
+            out=xw[:].bitcast(I32), in_=x_words[0].rearrange("p c r -> p (c r)").bitcast(I32)
+        )
+        for i in range(2):
+            nc.sync.dma_start(out=raw_w[i][:].bitcast(I32), in_=w_words[i][0].bitcast(I32))
+        for i in range(2):
+            load_scale_rows(nc.sync, raw_s[i], w_scales[i])
+        nc.sync.dma_start(out=ask1_t[:], in_=ask1)
+        nc.sync.dma_start(out=ask2_t[:], in_=ask2)
+        nc.gpsimd.dma_start(out=unit_t[:], in_=unit.rearrange("(p t) o -> p (t o)", t=PACK))
+        nc.sync.dma_start(out=raw_w[2][:].bitcast(I32), in_=w_words[2][0].bitcast(I32))
+        load_scale_rows(nc.sync, raw_s[2], w_scales[2])
+
+        size = keep.tile([P, PACK], F32, name="size")
+        sign = keep.tile([P, PACK], BF16, name="sign")
+        nc.scalar.activation(size[:], unit_t[:], ACT.Abs)
+        nc.scalar.activation(sign[:], unit_t[:], ACT.Sign)
+
+        xq_s = keep.tile([P, S], U8, name="xq_s", align_bytes=64)
+        xq_w = keep.tile([P, S], U32, name="xq_w", align_bytes=64)
+        nc.vector.tensor_copy(xq_s[:], xs[:].indirect(offs_t[:]))
+        nc.vector.tensor_copy(xq_w[:], xw[:].indirect(offs_t[:]))
+
+        def deal(i):
+            words = keep.tile([P, 2 * N], U8, name="dealt_w", tag="dealt_w%d" % (i % 2), align_bytes=64)
+            plane = keep.tile([P, N], U8, name="dealt_s", tag="dealt_s%d" % (i % 2), align_bytes=64)
+            nc.vector.tensor_copy(
+                words[:].rearrange("p (t m b) -> p t m b", t=PACK, b=2),
+                raw_w[i][:].rearrange("p (m t b) -> p t m b", t=PACK, b=2),
+            )
+            nc.vector.tensor_copy(
+                plane[:].rearrange("p (t m) -> p t m", t=PACK),
+                raw_s[i][:].rearrange("p (m t) -> p t m", t=PACK),
+            )
+            return words, plane
+
+        dealt = [deal(i) for i in range(2)]
+
+        def product(acc, i, t, codes, plane):
+            words, scales = dealt[i]
+            nc.tensor.matmul_mx(
+                out=acc,
+                lhsT=words[:, 2 * P * t : 2 * P * (t + 1)].bitcast(FP4X4),
+                lhsT_scale=scales[:, P * t : P * (t + 1)],
+                rhs=codes.bitcast(FP8X4),
+                rhs_scale=plane,
+                start=True,
+                stop=True,
+            )
+
+        y = []
+        z = []
+        for t in range(PACK):
+            acc_y = psum.tile([P, S], F32, name="acc_y", tag="bank%d" % (2 * t))
+            acc_z = psum.tile([P, S], F32, name="acc_z", tag="bank%d" % (2 * t + 1))
+            product(acc_y[:], 0, t, xq_w[:], xq_s[:])
+            product(acc_z[:], 1, t, xq_w[:], xq_s[:])
+            y_t = keep.tile([P, S], F32, name="y%d" % t)
+            z_t = keep.tile([P, S], F32, name="z%d" % t)
+            nc.scalar.activation(y_t[:], acc_y[:], ACT.Copy, scale=size[:, t : t + 1])
+            nc.vector.tensor_scalar(z_t[:], acc_z[:], size[:, t : t + 1], None, ALU.mult)
+            y.append(y_t)
+            z.append(z_t)
+
+        dealt.append(deal(2))
+        out_rows = out_0.rearrange("(p t) r -> p t r", t=PACK)
+        out_words = out_1[0].rearrange("p c r -> p (c r)").bitcast(I32)
+        out_plane = keep.tile([P, U], U8, name="out_plane", align_bytes=64)
+
+        def quote(r0, w):
+            cols = slice(r0 // LANES, (r0 + w) // LANES)
+            first = ring.tile([P, PACK, w], F32, name="first", tag="first")
+            second = ring.tile([P, PACK, w], F32, name="second", tag="second")
+            for t in range(PACK):
+                ya = ring.tile([P, w], F32, name="ya", tag="ya%d" % t)
+                yb = ring.tile([P, w], F32, name="yb", tag="yb%d" % t)
+                nc.scalar.activation(ya[:], y[t][:].indirect(ask1_t[:, cols]), ACT.Copy)
+                nc.scalar.activation(yb[:], y[t][:].indirect(ask2_t[:, cols]), ACT.Copy)
+                nc.vector.tensor_tensor(first[:, t, :], z[t][:].indirect(ask2_t[:, cols]), ya[:], ALU.add)
+                nc.vector.tensor_tensor(second[:, t, :], z[t][:].indirect(ask1_t[:, cols]), yb[:], ALU.add)
+            least = ring.tile([P, w, PACK], BF16, name="least", tag="least", align_bytes=64)
+            nc.vector.tensor_tensor(
+                least[:].rearrange("p (c i) t -> p c t i", i=RUN),
+                first[:].rearrange("p t (c i) -> p c t i", i=RUN),
+                second[:].rearrange("p t (c i) -> p c t i", i=RUN),
+                ALU.min,
+            )
+            hid = ring.tile([P, w, PACK], BF16, name="hid", tag="hid", align_bytes=64)
+            nc.vector.tensor_tensor(
+                hid[:], least[:], sign[:].unsqueeze(1).to_broadcast([P, w, PACK]), ALU.mult
+            )
+            codes = ring.tile([P, w], U32, name="codes", tag="codes", align_bytes=64)
+            plane = ring.tile([P, w], U8, name="plane", tag="plane", align_bytes=64)
+            nc.vector.quantize_mx(
+                out=codes[:].bitcast(FP8X4), scales=plane[:], in_=hid[:].rearrange("p c t -> p (c t)")
+            )
+            return codes, plane
+
+        def books(r0, w, codes, plane):
+            res = ring.tile([P, PACK, w], F32, name="res", tag="res")
+            rounded = ring.tile([P, w, PACK], BF16, name="rounded", tag="rounded", align_bytes=64)
+            for c0 in range(0, w, UNIT):
+                bank = ((r0 + c0) // UNIT) % 8
+                acc = psum.tile([P, PACK, UNIT], F32, name="acc", tag="bank%d" % bank)
+                for t in range(PACK):
+                    product(acc[:, t, :], 2, t, codes[:, c0 : c0 + UNIT], plane[:, c0 : c0 + UNIT])
+                nc.scalar.copy(rounded[:, c0 : c0 + UNIT, :], acc[:].rearrange("p t c -> p c t"))
+                nc.scalar.copy(res[:, :, c0 : c0 + UNIT], acc[:])
+            nc.sync.dma_start(out=out_rows[:, :, r0 : r0 + w], in_=res[:])
+            words = ring.tile([P, w], U32, name="words", tag="words", align_bytes=64)
+            nc.vector.quantize_mx(
+                out=words[:].bitcast(FP8X4),
+                scales=out_plane[:, r0 : r0 + w],
+                in_=rounded[:].rearrange("p c t -> p (c t)"),
+            )
+            nc.sync.dma_start(out=out_words[:, r0 : r0 + w], in_=words[:].bitcast(I32))
+
+        r0 = 0
+        last = None
+        for w in CHUNKS:
+            made = quote(r0, w)
+            if last is not None:
+                books(*last)
+            last = (r0, w) + made
+            r0 = r0 + w
+        books(*last)
+        for q in range(4):
+            nc.sync.dma_start(
+                out=out_2[0, 4 * q : 4 * q + 4, :].bitcast(I32),
+                in_=out_plane[32 * q : 32 * q + 4, :].bitcast(I32),
+            )

@@ -20,8 +20,13 @@ P = 128
 PACK = 4
 LANES = 16
 UNIT = 128
-CHUNKS = (256, 256, 256, 128, 128)
+CHUNKS = (512, 384, 128)
+HALF = 512
+SPARE = 32
 RUN = 2
+CAST_RUN = 4
+MOVED = (2, 3)
+VECTOR_CASTS_FROM = 640
 
 
 def tile_picked_ypeerlo_cmb_po_kernel(
@@ -54,24 +59,31 @@ def tile_picked_ypeerlo_cmb_po_kernel(
         w_scales = (w1_scales, w2_scales, w3_scales)
         unit_t = keep.tile([P, PACK], F32, name="unit_t")
 
+        y = [keep.tile([P, S + SPARE], F32, name="y%d" % t) for t in range(PACK)]
+        z = [keep.tile([P, S + SPARE], F32, name="z%d" % t) for t in range(PACK)]
+
         nc.vector.memset(xs[:].bitcast(I32), 0)
         for i in range(3):
             nc.vector.memset(raw_s[i][:].bitcast(I32), 0)
+        for t in range(PACK):
+            nc.vector.memset(y[t][:, S:], 0.0)
+            nc.vector.memset(z[t][:, S:], 0.0)
+
+        def load_weight(i):
+            nc.sync.dma_start(out=raw_w[i][:].bitcast(I32), in_=w_words[i][0].bitcast(I32))
+            load_scale_rows(nc.sync, raw_s[i], w_scales[i])
 
         nc.sync.dma_start(out=offs_t[:], in_=offs)
         load_scale_rows(nc.sync, xs, x_scales)
         nc.sync.dma_start(
             out=xw[:].bitcast(I32), in_=x_words[0].rearrange("p c r -> p (c r)").bitcast(I32)
         )
-        for i in range(2):
-            nc.sync.dma_start(out=raw_w[i][:].bitcast(I32), in_=w_words[i][0].bitcast(I32))
-        for i in range(2):
-            load_scale_rows(nc.sync, raw_s[i], w_scales[i])
+        load_weight(0)
+        nc.sync.dma_start(out=unit_t[:], in_=unit.rearrange("(p t) o -> p (t o)", t=PACK))
+        load_weight(1)
         nc.sync.dma_start(out=ask1_t[:], in_=ask1)
         nc.sync.dma_start(out=ask2_t[:], in_=ask2)
-        nc.gpsimd.dma_start(out=unit_t[:], in_=unit.rearrange("(p t) o -> p (t o)", t=PACK))
-        nc.sync.dma_start(out=raw_w[2][:].bitcast(I32), in_=w_words[2][0].bitcast(I32))
-        load_scale_rows(nc.sync, raw_s[2], w_scales[2])
+        load_weight(2)
 
         size = keep.tile([P, PACK], F32, name="size")
         sign = keep.tile([P, PACK], BF16, name="sign")
@@ -83,20 +95,26 @@ def tile_picked_ypeerlo_cmb_po_kernel(
         nc.vector.tensor_copy(xq_s[:], xs[:].indirect(offs_t[:]))
         nc.vector.tensor_copy(xq_w[:], xw[:].indirect(offs_t[:]))
 
-        def deal(i):
+        def dealt_tiles(i):
             words = keep.tile([P, 2 * N], U8, name="dealt_w", tag="dealt_w%d" % (i % 2), align_bytes=64)
             plane = keep.tile([P, N], U8, name="dealt_s", tag="dealt_s%d" % (i % 2), align_bytes=64)
-            nc.vector.tensor_copy(
-                words[:].rearrange("p (t m b) -> p t m b", t=PACK, b=2),
-                raw_w[i][:].rearrange("p (m t b) -> p t m b", t=PACK, b=2),
-            )
-            nc.vector.tensor_copy(
-                plane[:].rearrange("p (t m) -> p t m", t=PACK),
-                raw_s[i][:].rearrange("p (m t) -> p t m", t=PACK),
-            )
             return words, plane
 
-        dealt = [deal(i) for i in range(2)]
+        def deal(i, t0, t1):
+            words, plane = dealt[i]
+            nc.vector.tensor_copy(
+                words[:].rearrange("p (t m b) -> p t m b", t=PACK, b=2)[:, t0:t1],
+                raw_w[i][:].rearrange("p (m t b) -> p t m b", t=PACK, b=2)[:, t0:t1],
+            )
+            nc.vector.tensor_copy(
+                plane[:].rearrange("p (t m) -> p t m", t=PACK)[:, t0:t1],
+                raw_s[i][:].rearrange("p (m t) -> p t m", t=PACK)[:, t0:t1],
+            )
+
+        dealt = [dealt_tiles(i) for i in range(2)]
+        for t0, t1 in ((0, 1), (1, PACK)):
+            for i in range(2):
+                deal(i, t0, t1)
 
         def product(acc, i, t, codes, plane):
             words, scales = dealt[i]
@@ -110,36 +128,50 @@ def tile_picked_ypeerlo_cmb_po_kernel(
                 stop=True,
             )
 
-        y = []
-        z = []
         for t in range(PACK):
             acc_y = psum.tile([P, S], F32, name="acc_y", tag="bank%d" % (2 * t))
             acc_z = psum.tile([P, S], F32, name="acc_z", tag="bank%d" % (2 * t + 1))
             product(acc_y[:], 0, t, xq_w[:], xq_s[:])
             product(acc_z[:], 1, t, xq_w[:], xq_s[:])
-            y_t = keep.tile([P, S], F32, name="y%d" % t)
-            z_t = keep.tile([P, S], F32, name="z%d" % t)
-            nc.scalar.activation(y_t[:], acc_y[:], ACT.Copy, scale=size[:, t : t + 1])
-            nc.vector.tensor_scalar(z_t[:], acc_z[:], size[:, t : t + 1], None, ALU.mult)
-            y.append(y_t)
-            z.append(z_t)
+            nc.scalar.activation(y[t][:, :S], acc_y[:], ACT.Copy, scale=size[:, t : t + 1])
+            if t < PACK - 1:
+                nc.vector.tensor_scalar(z[t][:, :S], acc_z[:], size[:, t : t + 1], None, ALU.mult)
+            else:
+                nc.scalar.activation(z[t][:, :S], acc_z[:], ACT.Copy, scale=size[:, t : t + 1])
 
-        dealt.append(deal(2))
+        dealt.append(dealt_tiles(2))
+        deal(2, 0, PACK)
         out_rows = out_0.rearrange("(p t) r -> p t r", t=PACK)
         out_words = out_1[0].rearrange("p c r -> p (c r)").bitcast(I32)
         out_plane = keep.tile([P, U], U8, name="out_plane", align_bytes=64)
 
+        ya = [keep.tile([P, PACK, HALF], F32, name="ya%d" % h) for h in range(U // HALF)]
+        yb = [keep.tile([P, PACK, HALF], F32, name="yb%d" % h) for h in range(U // HALF)]
+
+        za = {t: keep.tile([P, HALF], F32, name="za%d" % t) for t in MOVED}
+
+        def fetch(h):
+            cols = slice(h * HALF // LANES, (h + 1) * HALF // LANES)
+            for t in range(PACK):
+                nc.scalar.activation(ya[h][:, t, :], y[t][:].indirect(ask1_t[:, cols]), ACT.Copy)
+                nc.scalar.activation(yb[h][:, t, :], y[t][:].indirect(ask2_t[:, cols]), ACT.Copy)
+                if h == 1 and t in MOVED:
+                    nc.scalar.activation(za[t][:], z[t][:].indirect(ask1_t[:, cols]), ACT.Copy)
+
         def quote(r0, w):
+            h, c0 = divmod(r0, HALF)
             cols = slice(r0 // LANES, (r0 + w) // LANES)
             first = ring.tile([P, PACK, w], F32, name="first", tag="first")
             second = ring.tile([P, PACK, w], F32, name="second", tag="second")
             for t in range(PACK):
-                ya = ring.tile([P, w], F32, name="ya", tag="ya%d" % t)
-                yb = ring.tile([P, w], F32, name="yb", tag="yb%d" % t)
-                nc.scalar.activation(ya[:], y[t][:].indirect(ask1_t[:, cols]), ACT.Copy)
-                nc.scalar.activation(yb[:], y[t][:].indirect(ask2_t[:, cols]), ACT.Copy)
-                nc.vector.tensor_tensor(first[:, t, :], z[t][:].indirect(ask2_t[:, cols]), ya[:], ALU.add)
-                nc.vector.tensor_tensor(second[:, t, :], z[t][:].indirect(ask1_t[:, cols]), yb[:], ALU.add)
+                nc.vector.tensor_tensor(
+                    first[:, t, :], z[t][:].indirect(ask2_t[:, cols]), ya[h][:, t, c0 : c0 + w], ALU.add
+                )
+                if h == 1 and t in MOVED:
+                    bids = za[t][:, c0 : c0 + w]
+                else:
+                    bids = z[t][:].indirect(ask1_t[:, cols])
+                nc.vector.tensor_tensor(second[:, t, :], bids, yb[h][:, t, c0 : c0 + w], ALU.add)
             least = ring.tile([P, w, PACK], BF16, name="least", tag="least", align_bytes=64)
             nc.vector.tensor_tensor(
                 least[:].rearrange("p (c i) t -> p c t i", i=RUN),
@@ -166,8 +198,14 @@ def tile_picked_ypeerlo_cmb_po_kernel(
                 acc = psum.tile([P, PACK, UNIT], F32, name="acc", tag="bank%d" % bank)
                 for t in range(PACK):
                     product(acc[:, t, :], 2, t, codes[:, c0 : c0 + UNIT], plane[:, c0 : c0 + UNIT])
-                nc.scalar.copy(rounded[:, c0 : c0 + UNIT, :], acc[:].rearrange("p t c -> p c t"))
+                if r0 + c0 < VECTOR_CASTS_FROM:
+                    nc.scalar.copy(rounded[:, c0 : c0 + UNIT, :], acc[:].rearrange("p t c -> p c t"))
                 nc.scalar.copy(res[:, :, c0 : c0 + UNIT], acc[:])
+                if r0 + c0 >= VECTOR_CASTS_FROM:
+                    nc.vector.tensor_copy(
+                        rounded[:, c0 : c0 + UNIT, :].rearrange("p (c i) t -> p c t i", i=CAST_RUN),
+                        res[:, :, c0 : c0 + UNIT].rearrange("p t (c i) -> p c t i", i=CAST_RUN),
+                    )
             nc.sync.dma_start(out=out_rows[:, :, r0 : r0 + w], in_=res[:])
             words = ring.tile([P, w], U32, name="words", tag="words", align_bytes=64)
             nc.vector.quantize_mx(
@@ -178,16 +216,13 @@ def tile_picked_ypeerlo_cmb_po_kernel(
             nc.sync.dma_start(out=out_words[:, r0 : r0 + w], in_=words[:].bitcast(I32))
 
         r0 = 0
-        last = None
         for w in CHUNKS:
-            made = quote(r0, w)
-            if last is not None:
-                books(*last)
-            last = (r0, w) + made
+            if r0 % HALF == 0:
+                fetch(r0 // HALF)
+            books(r0, w, *quote(r0, w))
             r0 = r0 + w
-        books(*last)
         for q in range(4):
-            nc.sync.dma_start(
+            (nc.sync, nc.scalar)[q % 2].dma_start(
                 out=out_2[0, 4 * q : 4 * q + 4, :].bitcast(I32),
                 in_=out_plane[32 * q : 32 * q + 4, :].bitcast(I32),
             )

@@ -24,9 +24,8 @@ CHUNKS = (512, 384, 128)
 HALF = 512
 SPARE = 32
 RUN = 2
-CAST_RUN = 4
 MOVED = (2, 3)
-VECTOR_CASTS_FROM = 640
+VECTOR_CASTS_FROM = 768
 
 
 def tile_picked_ypeerlo_cmb_po_kernel(
@@ -69,21 +68,23 @@ def tile_picked_ypeerlo_cmb_po_kernel(
             nc.vector.memset(y[t][:, S:], 0.0)
             nc.vector.memset(z[t][:, S:], 0.0)
 
-        def load_weight(i):
+        def load_words(i):
             nc.sync.dma_start(out=raw_w[i][:].bitcast(I32), in_=w_words[i][0].bitcast(I32))
-            load_scale_rows(nc.sync, raw_s[i], w_scales[i])
 
         nc.sync.dma_start(out=offs_t[:], in_=offs)
         load_scale_rows(nc.sync, xs, x_scales)
+        load_words(0)
         nc.sync.dma_start(
             out=xw[:].bitcast(I32), in_=x_words[0].rearrange("p c r -> p (c r)").bitcast(I32)
         )
-        load_weight(0)
+        load_scale_rows(nc.sync, raw_s[0], w_scales[0])
         nc.sync.dma_start(out=unit_t[:], in_=unit.rearrange("(p t) o -> p (t o)", t=PACK))
-        load_weight(1)
+        load_words(1)
+        load_scale_rows(nc.sync, raw_s[1], w_scales[1])
         nc.sync.dma_start(out=ask1_t[:], in_=ask1)
         nc.sync.dma_start(out=ask2_t[:], in_=ask2)
-        load_weight(2)
+        load_words(2)
+        load_scale_rows(nc.sync, raw_s[2], w_scales[2])
 
         size = keep.tile([P, PACK], F32, name="size")
         sign = keep.tile([P, PACK], BF16, name="sign")
@@ -95,33 +96,33 @@ def tile_picked_ypeerlo_cmb_po_kernel(
         nc.vector.tensor_copy(xq_s[:], xs[:].indirect(offs_t[:]))
         nc.vector.tensor_copy(xq_w[:], xw[:].indirect(offs_t[:]))
 
-        def dealt_tiles(i):
-            words = keep.tile([P, 2 * N], U8, name="dealt_w", tag="dealt_w%d" % (i % 2), align_bytes=64)
-            plane = keep.tile([P, N], U8, name="dealt_s", tag="dealt_s%d" % (i % 2), align_bytes=64)
-            return words, plane
+        dealt = {}
 
-        def deal(i, t0, t1):
-            words, plane = dealt[i]
-            nc.vector.tensor_copy(
-                words[:].rearrange("p (t m b) -> p t m b", t=PACK, b=2)[:, t0:t1],
+        def deal(engine, i, t0, t1, tag):
+            n = t1 - t0
+            words = keep.tile([P, n, 2 * P], U8, name="dealt_w", tag="w" + tag, align_bytes=64)
+            plane = keep.tile([P, n, P], U8, name="dealt_s", tag="s" + tag, align_bytes=64)
+            engine.tensor_copy(
+                words[:].rearrange("p t (m b) -> p t m b", b=2),
                 raw_w[i][:].rearrange("p (m t b) -> p t m b", t=PACK, b=2)[:, t0:t1],
             )
-            nc.vector.tensor_copy(
-                plane[:].rearrange("p (t m) -> p t m", t=PACK)[:, t0:t1],
-                raw_s[i][:].rearrange("p (m t) -> p t m", t=PACK)[:, t0:t1],
+            engine.tensor_copy(
+                plane[:], raw_s[i][:].rearrange("p (m t) -> p t m", t=PACK)[:, t0:t1]
             )
+            for t in range(t0, t1):
+                dealt[i, t] = (words[:, t - t0, :], plane[:, t - t0, :])
 
-        dealt = [dealt_tiles(i) for i in range(2)]
-        for t0, t1 in ((0, 1), (1, PACK)):
-            for i in range(2):
-                deal(i, t0, t1)
+        deal(nc.gpsimd, 0, 0, 1, "a")
+        deal(nc.gpsimd, 0, 1, PACK, "b")
+        deal(nc.vector, 1, 0, PACK, "c")
+        deal(nc.vector, 2, 0, PACK, "d")
 
         def product(acc, i, t, codes, plane):
-            words, scales = dealt[i]
+            words, scales = dealt[i, t]
             nc.tensor.matmul_mx(
                 out=acc,
-                lhsT=words[:, 2 * P * t : 2 * P * (t + 1)].bitcast(FP4X4),
-                lhsT_scale=scales[:, P * t : P * (t + 1)],
+                lhsT=words.bitcast(FP4X4),
+                lhsT_scale=scales,
                 rhs=codes.bitcast(FP8X4),
                 rhs_scale=plane,
                 start=True,
@@ -139,8 +140,6 @@ def tile_picked_ypeerlo_cmb_po_kernel(
             else:
                 nc.scalar.activation(z[t][:, :S], acc_z[:], ACT.Copy, scale=size[:, t : t + 1])
 
-        dealt.append(dealt_tiles(2))
-        deal(2, 0, PACK)
         out_rows = out_0.rearrange("(p t) r -> p t r", t=PACK)
         out_words = out_1[0].rearrange("p c r -> p (c r)").bitcast(I32)
         out_plane = keep.tile([P, U], U8, name="out_plane", align_bytes=64)
@@ -198,15 +197,16 @@ def tile_picked_ypeerlo_cmb_po_kernel(
                 acc = psum.tile([P, PACK, UNIT], F32, name="acc", tag="bank%d" % bank)
                 for t in range(PACK):
                     product(acc[:, t, :], 2, t, codes[:, c0 : c0 + UNIT], plane[:, c0 : c0 + UNIT])
+                cols = slice(c0, c0 + UNIT)
                 if r0 + c0 < VECTOR_CASTS_FROM:
-                    nc.scalar.copy(rounded[:, c0 : c0 + UNIT, :], acc[:].rearrange("p t c -> p c t"))
-                nc.scalar.copy(res[:, :, c0 : c0 + UNIT], acc[:])
-                if r0 + c0 >= VECTOR_CASTS_FROM:
-                    nc.vector.tensor_copy(
-                        rounded[:, c0 : c0 + UNIT, :].rearrange("p (c i) t -> p c t i", i=CAST_RUN),
-                        res[:, :, c0 : c0 + UNIT].rearrange("p t (c i) -> p c t i", i=CAST_RUN),
-                    )
-            nc.sync.dma_start(out=out_rows[:, :, r0 : r0 + w], in_=res[:])
+                    nc.scalar.copy(rounded[:, cols, :], acc[:].rearrange("p t c -> p c t"))
+                else:
+                    nc.vector.tensor_copy(rounded[:, cols, :], acc[:].rearrange("p t c -> p c t"))
+                nc.scalar.copy(res[:, :, cols], acc[:])
+                if r0 > 0:
+                    nc.sync.dma_start(out=out_rows[:, :, r0 + c0 : r0 + c0 + UNIT], in_=res[:, :, cols])
+            if r0 == 0:
+                nc.sync.dma_start(out=out_rows[:, :, r0 : r0 + w], in_=res[:])
             words = ring.tile([P, w], U32, name="words", tag="words", align_bytes=64)
             nc.vector.quantize_mx(
                 out=words[:].bitcast(FP8X4),

from contextlib import ExitStack

import concourse.mybir as mybir

K, T, S, N, H, U = 512, 1024, 512, 512, 512, 1024
FLOPS = 2 * K * N * S * 2 + 2 * H * N * U

F32 = mybir.dt.float32
BF16 = mybir.dt.bfloat16
I32 = mybir.dt.int32
U32 = mybir.dt.uint32
U16 = mybir.dt.uint16
U8 = mybir.dt.uint8
FP8X4 = mybir.dt.float8_e4m3fn_x4
FP4X4 = mybir.dt.float4_e2m1fn_x4
ALU = mybir.AluOpType
ACT = mybir.ActivationFunctionType

P = 128
PACK = 4
LANES = 16
UNIT = 128
CHUNKS = (512, 384, 128)
HALF = 512
SPARE = 32
RUN = 2
MOVED = (2, 3)
VECTOR_CASTS_FROM = 768


def tile_picked_ypeerlo_cmb_po_kernel(
    tc, x_words, x_scales, w1_words, w1_scales, w2_words, w2_scales, unit, w3_words, w3_scales,
    offs, ask1, ask2, out_0, out_1, out_2,
):
    nc = tc.nc
    with ExitStack() as ctx:
        lists = ctx.enter_context(tc.tile_pool(name="lists", bufs=1))
        keep = ctx.enter_context(tc.tile_pool(name="keep", bufs=1))
        ring = ctx.enter_context(tc.tile_pool(name="ring", bufs=2))
        psum = ctx.enter_context(tc.psum_pool(name="psum", bufs=1))

        def load_scale_rows(queue, plane, rows):
            for q in range(4):
                queue.dma_start(
                    out=plane[32 * q : 32 * q + 4, :].bitcast(I32),
                    in_=rows[0, 4 * q : 4 * q + 4, :].bitcast(I32),
                )

        offs_t = lists.tile([P, S // LANES], U16, name="offs_t")
        ask1_t = lists.tile([P, U // LANES], U16, name="ask1_t")
        ask2_t = lists.tile([P, U // LANES], U16, name="ask2_t")

        xw = keep.tile([P, T], U32, name="xw", align_bytes=64)
        xs = keep.tile([P, T], U8, name="xs", align_bytes=64)
        raw_w = [keep.tile([P, 2 * N], U8, name="raw_w%d" % i, align_bytes=64) for i in range(3)]
        raw_s = [keep.tile([P, N], U8, name="raw_s%d" % i, align_bytes=64) for i in range(3)]
        w_words = (w1_words, w2_words, w3_words)
        w_scales = (w1_scales, w2_scales, w3_scales)
        unit_t = keep.tile([P, PACK], F32, name="unit_t")

        y = [keep.tile([P, S + SPARE], F32, name="y%d" % t) for t in range(PACK)]
        z = [keep.tile([P, S + SPARE], F32, name="z%d" % t) for t in range(PACK)]

        nc.vector.memset(xs[:].bitcast(I32), 0)
        for i in range(3):
            nc.vector.memset(raw_s[i][:].bitcast(I32), 0)
        for t in range(PACK):
            nc.vector.memset(y[t][:, S:], 0.0)
            nc.vector.memset(z[t][:, S:], 0.0)

        def load_words(i):
            nc.sync.dma_start(out=raw_w[i][:].bitcast(I32), in_=w_words[i][0].bitcast(I32))

        nc.sync.dma_start(out=offs_t[:], in_=offs)
        load_scale_rows(nc.sync, xs, x_scales)
        load_words(0)
        nc.sync.dma_start(
            out=xw[:].bitcast(I32), in_=x_words[0].rearrange("p c r -> p (c r)").bitcast(I32)
        )
        load_scale_rows(nc.sync, raw_s[0], w_scales[0])
        nc.sync.dma_start(out=unit_t[:], in_=unit.rearrange("(p t) o -> p (t o)", t=PACK))
        load_words(1)
        load_scale_rows(nc.sync, raw_s[1], w_scales[1])
        nc.sync.dma_start(out=ask1_t[:], in_=ask1)
        nc.sync.dma_start(out=ask2_t[:], in_=ask2)
        load_words(2)
        load_scale_rows(nc.sync, raw_s[2], w_scales[2])

        size = keep.tile([P, PACK], F32, name="size")
        sign = keep.tile([P, PACK], BF16, name="sign")
        nc.scalar.activation(size[:], unit_t[:], ACT.Abs)
        nc.scalar.activation(sign[:], unit_t[:], ACT.Sign)

        xq_s = keep.tile([P, S], U8, name="xq_s", align_bytes=64)
        xq_w = keep.tile([P, S], U32, name="xq_w", align_bytes=64)
        nc.vector.tensor_copy(xq_s[:], xs[:].indirect(offs_t[:]))
        nc.vector.tensor_copy(xq_w[:], xw[:].indirect(offs_t[:]))

        dealt = {}

        def deal(engine, i, t0, t1, tag):
            n = t1 - t0
            words = keep.tile([P, n, 2 * P], U8, name="dealt_w", tag="w" + tag, align_bytes=64)
            plane = keep.tile([P, n, P], U8, name="dealt_s", tag="s" + tag, align_bytes=64)
            engine.tensor_copy(
                words[:].rearrange("p t (m b) -> p t m b", b=2),
                raw_w[i][:].rearrange("p (m t b) -> p t m b", t=PACK, b=2)[:, t0:t1],
            )
            engine.tensor_copy(
                plane[:], raw_s[i][:].rearrange("p (m t) -> p t m", t=PACK)[:, t0:t1]
            )
            for t in range(t0, t1):
                dealt[i, t] = (words[:, t - t0, :], plane[:, t - t0, :])

        deal(nc.gpsimd, 0, 0, 1, "a")
        deal(nc.gpsimd, 0, 1, PACK, "b")
        deal(nc.vector, 1, 0, PACK, "c")
        deal(nc.vector, 2, 0, PACK, "d")

        def product(acc, i, t, codes, plane):
            words, scales = dealt[i, t]
            nc.tensor.matmul_mx(
                out=acc,
                lhsT=words.bitcast(FP4X4),
                lhsT_scale=scales,
                rhs=codes.bitcast(FP8X4),
                rhs_scale=plane,
                start=True,
                stop=True,
            )

        for t in range(PACK):
            acc_y = psum.tile([P, S], F32, name="acc_y", tag="bank%d" % (2 * t))
            acc_z = psum.tile([P, S], F32, name="acc_z", tag="bank%d" % (2 * t + 1))
            product(acc_y[:], 0, t, xq_w[:], xq_s[:])
            product(acc_z[:], 1, t, xq_w[:], xq_s[:])
            nc.scalar.activation(y[t][:, :S], acc_y[:], ACT.Copy, scale=size[:, t : t + 1])
            if t < PACK - 1:
                nc.vector.tensor_scalar(z[t][:, :S], acc_z[:], size[:, t : t + 1], None, ALU.mult)
            else:
                nc.scalar.activation(z[t][:, :S], acc_z[:], ACT.Copy, scale=size[:, t : t + 1])

        out_rows = out_0.rearrange("(p t) r -> p t r", t=PACK)
        out_words = out_1[0].rearrange("p c r -> p (c r)").bitcast(I32)
        out_plane = keep.tile([P, U], U8, name="out_plane", align_bytes=64)

        ya = [keep.tile([P, PACK, HALF], F32, name="ya%d" % h) for h in range(U // HALF)]
        yb = [keep.tile([P, PACK, HALF], F32, name="yb%d" % h) for h in range(U // HALF)]

        za = {t: keep.tile([P, HALF], F32, name="za%d" % t) for t in MOVED}

        def fetch(h):
            cols = slice(h * HALF // LANES, (h + 1) * HALF // LANES)
            for t in range(PACK):
                nc.scalar.activation(ya[h][:, t, :], y[t][:].indirect(ask1_t[:, cols]), ACT.Copy)
                nc.scalar.activation(yb[h][:, t, :], y[t][:].indirect(ask2_t[:, cols]), ACT.Copy)
                if h == 1 and t in MOVED:
                    nc.scalar.activation(za[t][:], z[t][:].indirect(ask1_t[:, cols]), ACT.Copy)

        def quote(r0, w):
            h, c0 = divmod(r0, HALF)
            cols = slice(r0 // LANES, (r0 + w) // LANES)
            first = ring.tile([P, PACK, w], F32, name="first", tag="first")
            second = ring.tile([P, PACK, w], F32, name="second", tag="second")
            for t in range(PACK):
                nc.vector.tensor_tensor(
                    first[:, t, :], z[t][:].indirect(ask2_t[:, cols]), ya[h][:, t, c0 : c0 + w], ALU.add
                )
                if h == 1 and t in MOVED:
                    bids = za[t][:, c0 : c0 + w]
                else:
                    bids = z[t][:].indirect(ask1_t[:, cols])
                nc.vector.tensor_tensor(second[:, t, :], bids, yb[h][:, t, c0 : c0 + w], ALU.add)
            least = ring.tile([P, w, PACK], BF16, name="least", tag="least", align_bytes=64)
            nc.vector.tensor_tensor(
                least[:].rearrange("p (c i) t -> p c t i", i=RUN),
                first[:].rearrange("p t (c i) -> p c t i", i=RUN),
                second[:].rearrange("p t (c i) -> p c t i", i=RUN),
                ALU.min,
            )
            hid = ring.tile([P, w, PACK], BF16, name="hid", tag="hid", align_bytes=64)
            nc.vector.tensor_tensor(
                hid[:], least[:], sign[:].unsqueeze(1).to_broadcast([P, w, PACK]), ALU.mult
            )
            codes = ring.tile([P, w], U32, name="codes", tag="codes", align_bytes=64)
            plane = ring.tile([P, w], U8, name="plane", tag="plane", align_bytes=64)
            nc.vector.quantize_mx(
                out=codes[:].bitcast(FP8X4), scales=plane[:], in_=hid[:].rearrange("p c t -> p (c t)")
            )
            return codes, plane

        def books(r0, w, codes, plane):
            res = ring.tile([P, PACK, w], F32, name="res", tag="res")
            rounded = ring.tile([P, w, PACK], BF16, name="rounded", tag="rounded", align_bytes=64)
            for c0 in range(0, w, UNIT):
                bank = ((r0 + c0) // UNIT) % 8
                acc = psum.tile([P, PACK, UNIT], F32, name="acc", tag="bank%d" % bank)
                for t in range(PACK):
                    product(acc[:, t, :], 2, t, codes[:, c0 : c0 + UNIT], plane[:, c0 : c0 + UNIT])
                cols = slice(c0, c0 + UNIT)
                if r0 + c0 < VECTOR_CASTS_FROM:
                    nc.scalar.copy(rounded[:, cols, :], acc[:].rearrange("p t c -> p c t"))
                else:
                    nc.vector.tensor_copy(rounded[:, cols, :], acc[:].rearrange("p t c -> p c t"))
                nc.scalar.copy(res[:, :, cols], acc[:])
                if r0 > 0:
                    nc.sync.dma_start(out=out_rows[:, :, r0 + c0 : r0 + c0 + UNIT], in_=res[:, :, cols])
            if r0 == 0:
                nc.sync.dma_start(out=out_rows[:, :, r0 : r0 + w], in_=res[:])
            words = ring.tile([P, w], U32, name="words", tag="words", align_bytes=64)
            nc.vector.quantize_mx(
                out=words[:].bitcast(FP8X4),
                scales=out_plane[:, r0 : r0 + w],
                in_=rounded[:].rearrange("p c t -> p (c t)"),
            )
            nc.sync.dma_start(out=out_words[:, r0 : r0 + w], in_=words[:].bitcast(I32))

        r0 = 0
        for w in CHUNKS:
            if r0 % HALF == 0:
                fetch(r0 // HALF)
            books(r0, w, *quote(r0, w))
            r0 = r0 + w
        for q in range(4):
            (nc.sync, nc.scalar)[q % 2].dma_start(
                out=out_2[0, 4 * q : 4 * q + 4, :].bitcast(I32),
                in_=out_plane[32 * q : 32 * q + 4, :].bitcast(I32),
            )
